import numpy as np
import ml_dtypes


def mxq(x, axis, fmt="e4m3"):
    dtype, down = {"e4m3": (ml_dtypes.float8_e4m3fn, 7), "e5m2": (ml_dtypes.float8_e5m2, 14)}[fmt]
    v = np.moveaxis(np.asarray(x, np.float32).astype(ml_dtypes.bfloat16).astype(np.float64), axis, -1)
    blocks = v.reshape(v.shape[:-1] + (-1, 32))
    amax = np.abs(blocks).max(-1, keepdims=True)
    byte = np.maximum(np.where(amax > 0, np.frexp(amax)[1] - 1 + 127, 0) - down, 1)
    scale = np.exp2(byte - 127.0)
    codes = (blocks / scale).astype(np.float32).astype(dtype).astype(np.float64)
    return np.moveaxis((codes * scale).reshape(v.shape), -1, axis)


WIDE = False


def mx_kscale(k):
    if not WIDE:
        return np.ones(k)
    levels = np.array([10, -10, 5, -5, 0])
    if k % 512:
        return np.exp2(np.random.permutation(np.resize(levels, k // 32))).repeat(32)
    a = np.empty((k // 512, 16))
    for p in range(k // 512):
        a[p, :8] = np.random.permutation(np.resize(levels, 8))
        for g in range(8):
            far = levels[np.abs(levels - a[p, g]) >= 10]
            a[p, g + 8] = far[np.random.randint(len(far))]
    return np.exp2(a.ravel()).repeat(32)


def f64(x):
    return np.asarray(x).astype(np.float64)


def striped(idx):
    return np.tile(idx.reshape(-1, 16).T, (8, 1)).astype(np.uint16)


def unstriped(offs):
    return offs[:16].T.reshape(-1).astype(np.int64)


E2M1 = np.array([0.0, 0.5, 1.0, 1.5, 2.0, 3.0, 4.0, 6.0, -0.0, -0.5, -1.0, -1.5, -2.0, -3.0, -4.0, -6.0])


def pack_weight(w, fmt):
    k, n = w.shape
    w = f64(np.asarray(w, np.float32).astype(ml_dtypes.bfloat16)).reshape(k // 32, 32, n)
    amax = np.abs(w).max(1)
    if fmt == "e4m3":
        byte = np.frexp(amax)[1] - 1 + 127 - 7
    else:
        mant, ex = np.frexp(amax / 6.0)
        byte = np.where(mant > 0.5, ex, ex - 1) + 127
    byte = np.clip(np.where(amax > 0, byte, 1), 1, 254)
    scaled = (w * np.exp2(127.0 - byte)[:, None, :]).reshape(k, n).astype(np.float32)
    by_word = np.ascontiguousarray(scaled.reshape(k // 512, 128, 4, n).transpose(0, 1, 3, 2))
    if fmt == "e4m3":
        words = by_word.astype(ml_dtypes.float8_e4m3fn).view(np.uint8)
    else:
        c = by_word.astype(ml_dtypes.float4_e2m1fn).view(np.uint8) & 0xF
        words = (c[..., 0::2] | (c[..., 1::2] << 4)).reshape(k // 512, 128, 2 * n)
    return np.ascontiguousarray(words), np.ascontiguousarray(byte.astype(np.uint8).reshape(k // 512, 16, n))


def unpack_weight(words, scales, fmt):
    g, _, n = scales.shape
    words = np.ascontiguousarray(words).reshape(g, 128, n, -1)
    if fmt == "e4m3":
        vals = words.view(ml_dtypes.float8_e4m3fn).astype(np.float64)
    else:
        nib = np.empty((g, 128, n, 4), np.uint8)
        nib[..., 0::2] = words & 0xF
        nib[..., 1::2] = words >> 4
        vals = E2M1[nib]
    vals = vals * np.repeat(np.exp2(scales.astype(np.float64) - 127.0), 8, axis=1)[..., None]
    return vals.transpose(0, 1, 3, 2).reshape(g * 512, n)


def gelu(v):
    return 0.5 * v * (1.0 + np.tanh(np.sqrt(2.0 / np.pi) * (v + 0.044715 * v**3)))


K, H, N, T, S, T2, P = 1024, 512, 384, 4096, 1024, 2048, 1024

def setup_inputs():
    n = np.random.standard_normal
    s = mx_kscale(K)[:, None]
    u = mx_kscale(H)[:, None]
    tab_words, tab_scales = pack_weight(n((K, T)) * s, "e4m3")
    w1 = (0.5 * n((K, H)) / np.sqrt(K) / s).astype(np.float32)
    gain = (1.5 * np.exp(0.3 * n(H)) * u[:, 0]).astype(np.float32)
    state = (0.7 * n((H, T2)) * u).astype(np.float32)
    wa_words, wa_scales = pack_weight(0.6 * n((H, N)) / np.sqrt(H) / u, "e2m1")
    wb = (0.35 * n((H, N)) / np.sqrt(H) / (u * u)).astype(np.float32)
    rs = (1.5 * np.exp(0.3 * n(N))).astype(np.float32)
    wgs = np.exp(0.3 * n((128, S))).astype(np.float32)
    wgo = np.exp(0.3 * n((128, P))).astype(np.float32)
    return {"tab_words": tab_words, "tab_scales": tab_scales, "w1": w1, "gain": gain,
            "state": state, "wa_words": wa_words, "wa_scales": wa_scales, "wb": wb,
            "rs": rs, "wgs": wgs, "wgo": wgo,
            "offs": striped(np.random.permutation(T)[:S]),
            "offs2": striped(np.random.permutation(T2)[:S]),
            "offs3": striped(np.random.permutation(T2)[:P]),
            "offs4": striped(np.random.permutation(T2)[:P])}

def reference(tab_words, tab_scales, w1, gain, state, wa_words, wa_scales, wb, rs, wgs, wgo, offs, offs2, offs3, offs4):
    v = unpack_weight(tab_words, tab_scales, "e4m3")[:, unstriped(offs)]
    h = np.sin(mxq(f64(w1), 0, "e4m3").T @ v) * f64(gain)[:, None]
    page = np.zeros((H, T2))
    page[:, unstriped(offs2)] = np.tile(f64(wgs), (H // 128, 1)) * h
    z = page + f64(state)
    z2 = z * z
    wa = unpack_weight(wa_words, wa_scales, "e2m1")
    y = wa.T @ mxq(z, 0, "e4m3") + mxq(f64(wb), 0, "e4m3").T @ mxq(z2, 0, "e4m3")
    x = np.tanh(y[:, unstriped(offs3)]) * f64(rs)[:, None]
    out = np.zeros((N, T2))
    out[:, unstriped(offs4)] = np.tile(f64(wgo), (N // 128, 1)) * x
    return out

@@ -1,0 +1,274 @@
+import math
+from contextlib import ExitStack
+
+import concourse.mybir as mybir
+
+K, H, N, T, S, T2, PICKS = 1024, 512, 384, 4096, 1024, 2048, 1024
+FLOPS = 2 * K * H * S + 2 * 2 * H * N * T2
+
+F32 = mybir.dt.float32
+BF16 = mybir.dt.bfloat16
+I32 = mybir.dt.int32
+U32 = mybir.dt.uint32
+U16 = mybir.dt.uint16
+U8 = mybir.dt.uint8
+FP8X4 = mybir.dt.float8_e4m3fn_x4
+FP4X4 = mybir.dt.float4_e2m1fn_x4
+ACT = mybir.ActivationFunctionType
+ALU = mybir.AluOpType
+
+P = 128
+PACK = 4
+BANK = 512
+ROUNDER = 1.5 * 2.0**23
+TWO_PI = 2.0 * math.pi
+
+
+def tile_list_cheat_review_queue_kernel(
+    tc, tab_words, tab_scales, w1, gain, state, wa_words, wa_scales, wb, rs, wgs, wgo, offs, offs2, offs3, offs4, out
+):
+    nc = tc.nc
+    passes = K // (P * PACK)
+    halves = S // BANK
+    chunks = T2 // BANK
+    n_tiles = N // P
+
+    with ExitStack() as ctx:
+        lists = ctx.enter_context(tc.tile_pool(name="lists", bufs=1))
+        keep = ctx.enter_context(tc.tile_pool(name="keep", bufs=1))
+        ring = ctx.enter_context(tc.tile_pool(name="ring", bufs=2))
+        psum = ctx.enter_context(tc.psum_pool(name="psum", bufs=1))
+
+        def sb(name, shape, dtype, tag=None):
+            return keep.tile(shape, dtype, name=name, tag=tag or name, align_bytes=64)
+
+        def four_banks(b, name):
+            return psum.tile([P, 4, BANK], F32, name=name, tag="banks%d" % b)
+
+        idx = []
+        for n, src in enumerate((offs, offs2, offs3, offs4)):
+            tl = lists.tile([P, S // 16], U16, name="list%d" % n)
+            nc.sync.dma_start(tl[:], src)
+            idx.append(tl)
+        idx_tab, idx_page, idx_pick, idx_out = idx
+
+        tab = [sb("tab%d" % a, [P, T], U32) for a in range(passes)]
+
+        def load_tab(a):
+            nc.sync.dma_start(tab[a][:].bitcast(I32), tab_words[a].rearrange("p t i -> p (t i)").bitcast(I32))
+
+        load_tab(0)
+        tab_sc = sb("tab_sc", [P, T], U8)
+        nc.vector.memset(tab_sc[:].bitcast(I32), 0)
+        for q in range(4):
+            nc.gpsimd.dma_start(
+                tab_sc[32 * q : 32 * q + 4 * passes, :].bitcast(I32), tab_scales[:, 4 * q : 4 * q + 4, :].bitcast(I32)
+            )
+        w1_raw = [sb("w1_raw%d" % a, [P, PACK, H], F32, tag="big%d" % a) for a in range(passes)]
+        for a in range(passes):
+            nc.sync.dma_start(w1_raw[a][:], w1[a * 512 : (a + 1) * 512, :].rearrange("(p j) c -> p j c", j=PACK))
+        load_tab(1)
+
+        wgs_rows = wgs.rearrange("(m j) s -> m j s", j=PACK)
+        wg_first = sb("wg_first", [P, S], F32)
+        wg_rest = sb("wg_rest", [P, PACK - 1, S], F32)
+        for q in range(4):
+            nc.sync.dma_start(wg_first[32 * q : 32 * q + 32, :], wgs_rows[:, 0, :])
+        gain_sb = sb("gain_sb", [P, PACK], F32)
+        nc.sync.dma_start(gain_sb[:], gain.rearrange("(p j) -> p j", j=PACK))
+        for q in range(4):
+            nc.sync.dma_start(wg_rest[32 * q : 32 * q + 32, :, :], wgs_rows[:, 1:PACK, :])
+        wg = [wg_first[:]] + [wg_rest[:, j, :] for j in range(PACK - 1)]
+
+        state_rows = state.rearrange("(p j) t -> p j t", j=PACK)
+        z = [[sb("z%d_%d" % (u, c), [P, 2, BANK], F32) for c in range(chunks)] for u in range(2)]
+
+        def load_state(u):
+            for c in range(chunks):
+                nc.sync.dma_start(z[u][c][:], state_rows[:, 2 * u : 2 * u + 2, c * BANK : (c + 1) * BANK])
+
+        wb_raw = sb("wb_raw", [P, PACK, N], F32, tag="wb_raw")
+        nc.sync.dma_start(wb_raw[:], wb.rearrange("(p j) n -> p j n", j=PACK))
+        rs_sb = sb("rs_sb", [P, n_tiles], F32)
+        with nc.allow_non_contiguous_dma(reason="one value of rs to a partition"):
+            nc.sync.dma_start(rs_sb[:], rs.rearrange("(i p) -> p i", p=P))
+        wgo_sb = sb("wgo_sb", [P, PICKS], F32)
+        nc.sync.dma_start(wgo_sb[:], wgo)
+        load_state(0)
+        load_state(1)
+        wa_codes = sb("wa_codes", [P, 2 * N], U8)
+        nc.sync.dma_start(wa_codes[:].bitcast(I32), wa_words[0].bitcast(I32))
+        wa_sc = sb("wa_sc", [P, N], U8)
+        nc.vector.memset(wa_sc[:].bitcast(I32), 0)
+        for q in range(4):
+            nc.sync.dma_start(wa_sc[32 * q : 32 * q + 4, :].bitcast(I32), wa_scales[0, 4 * q : 4 * q + 4, :].bitcast(I32))
+
+        zero_in = sb("zero_in", [P, 1], F32)
+        zero = sb("zero", [P, 1], F32)
+        nc.vector.memset(zero_in[:], 0.0)
+        nc.scalar.activation(zero[:], zero_in[:], ACT.Silu)
+
+        pages = [sb("page%d" % b, [P, T2], F32) for b in range(2)]
+        outs = [sb("out%d" % b, [P, T2], F32) for b in range(2)]
+        for tl in pages + outs:
+            nc.vector.memset(tl[:], 0.0)
+
+        v_codes = [sb("v_codes0", [P, S], U32)]
+        v_sc = sb("v_sc", [P, S], U8)
+        nc.vector.tensor_copy(v_codes[0][:], tab[0][:].indirect(idx_tab[:]))
+        nc.vector.tensor_copy(v_sc[:], tab_sc[:].indirect(idx_tab[:]))
+
+        w1_codes = sb("w1_codes", [P, passes, H], U32)
+        w1_sc = sb("w1_sc", [P, passes, H], U8)
+        for a in range(passes):
+            w1_bf = sb("w1_bf%d" % a, [P, PACK * H], BF16, tag=("big2", "tab_sc")[a])
+            dst = w1_bf[:].rearrange("p (t m j) -> p m j t", t=PACK, j=PACK)
+            src = w1_raw[a][:].rearrange("p j (m t) -> p m j t", t=PACK)
+            if a == 0:
+                nc.scalar.copy(dst, src)
+            else:
+                nc.vector.tensor_copy(dst, src)
+            nc.vector.quantize_mx(w1_codes[:, a, :].bitcast(FP8X4), w1_sc[:, a, :], w1_bf[:])
+        v_codes.append(sb("v_codes1", [P, S], U32, tag="tab_sc"))
+
+        x_banks = [four_banks(u, "x%d" % u) for u in range(2)]
+        x = [[x_banks[j // 2][:, halves * (j % 2) + h, :] for h in range(halves)] for j in range(PACK)]
+
+        def stage1(a, j, h):
+            cols = slice(h * BANK, (h + 1) * BANK)
+            rows = slice(j * P, (j + 1) * P)
+            nc.tensor.matmul_mx(
+                x[j][h],
+                lhsT=w1_codes[:, a, rows].bitcast(FP8X4),
+                lhsT_scale=w1_sc[:, a, rows],
+                rhs=v_codes[a][:, cols].bitcast(FP8X4),
+                rhs_scale=v_sc[4 * a : P, cols],
+                start=(a == 0),
+                stop=(a == passes - 1),
+            )
+
+        for h in range(halves):
+            nc.vector.tensor_copy(
+                v_codes[1][:, h * BANK : (h + 1) * BANK], tab[1][:].indirect(idx_tab[:, h * 32 : (h + 1) * 32])
+            )
+            for j in range(PACK):
+                for a in range(passes):
+                    stage1(a, j, h)
+
+        sines = [sb("sine%d" % j, [P, S], F32, tag="slot%d" % j) for j in range(PACK)]
+
+        def sine(j, h):
+            turns = ring.tile([P, BANK], F32, name="turns", tag="ring_a", align_bytes=64)
+            whole = ring.tile([P, BANK], U32, name="whole", tag="ring_b", align_bytes=64)
+            nc.scalar.activation(turns[:], x[j][h], ACT.Copy, scale=1.0 / TWO_PI)
+            nc.scalar.activation(whole[:], turns[:], ACT.Copy, bias=ROUNDER)
+            nc.vector.scalar_tensor_tensor(
+                turns[:], whole[:].bitcast(I32), ROUNDER, turns[:], ALU.subtract, ALU.subtract
+            )
+            nc.scalar.activation(sines[j][:, h * BANK : (h + 1) * BANK], turns[:], ACT.Sin, bias=zero[:], scale=-TWO_PI)
+
+        def scatter(j, lo, hi):
+            nc.vector.tensor_tensor(
+                pages[j % 2][:].indirect(idx_page[:, lo // 16 : hi // 16]), sines[j][:, lo:hi], wg[j][:, lo:hi], ALU.mult
+            )
+
+        def add_state(j, c):
+            zj = z[j // 2][c][:, j % 2, :]
+            nc.vector.scalar_tensor_tensor(
+                zj, pages[j % 2][:, c * BANK : (c + 1) * BANK], gain_sb[:, j : j + 1], zj, ALU.mult, ALU.add
+            )
+
+        z_bf = [sb("z_bf%d" % c, [P, BANK, PACK], BF16) for c in range(chunks)]
+        zz_bf = [sb("zz_bf%d" % c, [P, BANK, PACK], BF16) for c in range(chunks)]
+
+        def round_pair(u, c):
+            src = z[u][c][:].rearrange("p j t -> p t j")
+            if u == 0:
+                nc.scalar.copy(z_bf[c][:, :, 0:2], src)
+            else:
+                nc.vector.tensor_copy(z_bf[c][:, :, 2:4], src)
+            nc.scalar.activation(zz_bf[c][:, :, 2 * u : 2 * u + 2], src, ACT.Square)
+
+        sine(0, 0)
+        sine(0, 1)
+        scatter(0, 0, BANK)
+        sine(1, 0)
+        sine(1, 1)
+        scatter(0, BANK, S)
+        for j in range(PACK - 1):
+            if j + 2 < PACK:
+                sine(j + 2, 0)
+                sine(j + 2, 1)
+            for c in range(chunks):
+                add_state(j, c)
+            scatter(j + 1, 0, S)
+            if j == 0:
+                wb_bf = sb("wb_bf", [P, N, PACK], BF16)
+                nc.scalar.copy(
+                    wb_bf[:].rearrange("p (c i) j -> p c j i", i=4), wb_raw[:].rearrange("p j (c i) -> p c j i", i=4)
+                )
+                wb_codes = sb("wb_codes", [P, N], U32)
+                wb_sc = sb("wb_sc", [P, N], U8)
+                wb_flat = wb_bf[:].rearrange("p n j -> p (n j)")
+                for lo, hi in ((0, 256), (256, N)):
+                    nc.vector.quantize_mx(
+                        wb_codes[:, lo:hi].bitcast(FP8X4), wb_sc[:, lo:hi], wb_flat[:, PACK * lo : PACK * hi]
+                    )
+                factor0 = sb("factor0", [P, PICKS], F32, tag="wb_raw")
+                nc.scalar.activation(factor0[:], wgo_sb[:], ACT.Copy, scale=rs_sb[:, 0:1])
+            if j == 1:
+                for c in range(chunks):
+                    round_pair(0, c)
+
+        codes = [sb("codes%d" % c, [P, 2, BANK], U32, tag="slot%d" % c) for c in range(chunks)]
+        scales = [sb("scales%d" % c, [P, 2, BANK], U8) for c in range(chunks)]
+        scores = [sb("score%d" % i, [P, T2], F32, tag="big%d" % i) for i in range(n_tiles)]
+
+        def stage2(i, c, y_banks):
+            acc = y_banks[:, c, :]
+            rows = slice(i * P, (i + 1) * P)
+            nc.tensor.matmul_mx(
+                acc,
+                lhsT=wa_codes[:, 2 * i * P : 2 * (i + 1) * P].bitcast(FP4X4),
+                lhsT_scale=wa_sc[:, rows],
+                rhs=codes[c][:, 0, :].bitcast(FP8X4),
+                rhs_scale=scales[c][:, 0, :],
+                start=True,
+                stop=False,
+            )
+            nc.tensor.matmul_mx(
+                acc,
+                lhsT=wb_codes[:, rows].bitcast(FP8X4),
+                lhsT_scale=wb_sc[:, rows],
+                rhs=codes[c][:, 1, :].bitcast(FP8X4),
+                rhs_scale=scales[c][:, 1, :],
+                start=False,
+                stop=True,
+            )
+            nc.scalar.activation(scores[i][:, c * BANK : (c + 1) * BANK], acc, ACT.Tanh, bias=zero[:])
+
+        y_banks = four_banks(0, "y0")
+        for c in range(chunks):
+            add_state(PACK - 1, c)
+            round_pair(1, c)
+            for u, src in enumerate((z_bf[c], zz_bf[c])):
+                nc.vector.quantize_mx(
+                    codes[c][:, u, :].bitcast(FP8X4), scales[c][:, u, :], src[:].rearrange("p t j -> p (t j)")
+                )
+            stage2(0, c, y_banks)
+        for i in range(1, n_tiles):
+            y_banks = four_banks(0, "y%d" % i)
+            for c in range(chunks):
+                stage2(i, c, y_banks)
+
+        factors = [factor0[:]]
+        for i in range(n_tiles):
+            picked = sb("picked%d" % i, [P, PICKS], F32, tag="z0_%d" % i)
+            nc.vector.tensor_copy(picked[:], scores[i][:].indirect(idx_pick[:]))
+            if i == 0:
+                factor_rest = sb("factor_rest", [P, n_tiles - 1, PICKS], F32, tag="big0")
+                for m in range(1, n_tiles):
+                    nc.scalar.activation(factor_rest[:, m - 1, :], wgo_sb[:], ACT.Copy, scale=rs_sb[:, m : m + 1])
+                    factors.append(factor_rest[:, m - 1, :])
+            nc.vector.tensor_tensor(outs[i % 2][:].indirect(idx_out[:]), picked[:], factors[i], ALU.mult)
+            nc.sync.dma_start(out[i * P : (i + 1) * P, :], outs[i % 2][:])

@@ -36,44 +36,44 @@ def tile_list_cheat_review_queue_kernel(
     with ExitStack() as ctx:
         lists = ctx.enter_context(tc.tile_pool(name="lists", bufs=1))
         keep = ctx.enter_context(tc.tile_pool(name="keep", bufs=1))
-        ring = ctx.enter_context(tc.tile_pool(name="ring", bufs=2))
+        ring = ctx.enter_context(tc.tile_pool(name="ring", bufs=6))
         psum = ctx.enter_context(tc.psum_pool(name="psum", bufs=1))
 
         def sb(name, shape, dtype, tag=None):
             return keep.tile(shape, dtype, name=name, tag=tag or name, align_bytes=64)
 
-        def four_banks(b, name):
-            return psum.tile([P, 4, BANK], F32, name=name, tag="banks%d" % b)
+        def bank(b, name):
+            return psum.tile([P, BANK], F32, name=name, tag="bank%d" % b)
 
-        idx = []
-        for n, src in enumerate((offs, offs2, offs3, offs4)):
-            tl = lists.tile([P, S // 16], U16, name="list%d" % n)
-            nc.sync.dma_start(tl[:], src)
-            idx.append(tl)
-        idx_tab, idx_page, idx_pick, idx_out = idx
+        idx_tab, idx_page, idx_pick, idx_out = [lists.tile([P, S // 16], U16, name="list%d" % n) for n in range(4)]
+        sc_rows = sb("sc_rows", [P, T // 4], I32, tag="slot3")
+        for q in range(4):
+            nc.sync.dma_start(
+                sc_rows[32 * q : 32 * q + 4 * passes, :], tab_scales[:, 4 * q : 4 * q + 4, :].bitcast(I32)
+            )
+        nc.sync.dma_start(idx_tab[:], offs)
 
         tab = [sb("tab%d" % a, [P, T], U32) for a in range(passes)]
 
         def load_tab(a):
             nc.sync.dma_start(tab[a][:].bitcast(I32), tab_words[a].rearrange("p t i -> p (t i)").bitcast(I32))
 
-        load_tab(0)
-        tab_sc = sb("tab_sc", [P, T], U8)
-        nc.vector.memset(tab_sc[:].bitcast(I32), 0)
-        for q in range(4):
-            nc.gpsimd.dma_start(
-                tab_sc[32 * q : 32 * q + 4 * passes, :].bitcast(I32), tab_scales[:, 4 * q : 4 * q + 4, :].bitcast(I32)
-            )
         w1_raw = [sb("w1_raw%d" % a, [P, PACK, H], F32, tag="big%d" % a) for a in range(passes)]
         for a in range(passes):
             nc.sync.dma_start(w1_raw[a][:], w1[a * 512 : (a + 1) * 512, :].rearrange("(p j) c -> p j c", j=PACK))
-        load_tab(1)
+            load_tab(a)
+        tab_sc = sb("tab_sc", [P, T], U8)
+        nc.vector.memset(tab_sc[:].bitcast(I32), 0)
+        for q in range(4):
+            rows = slice(32 * q, 32 * q + 4 * passes)
+            nc.vector.tensor_copy(tab_sc[rows, :].bitcast(I32), sc_rows[rows, :])
 
         wgs_rows = wgs.rearrange("(m j) s -> m j s", j=PACK)
         wg_first = sb("wg_first", [P, S], F32)
         wg_rest = sb("wg_rest", [P, PACK - 1, S], F32)
         for q in range(4):
             nc.sync.dma_start(wg_first[32 * q : 32 * q + 32, :], wgs_rows[:, 0, :])
+        nc.sync.dma_start(idx_page[:], offs2)
         gain_sb = sb("gain_sb", [P, PACK], F32)
         nc.sync.dma_start(gain_sb[:], gain.rearrange("(p j) -> p j", j=PACK))
         for q in range(4):
@@ -81,11 +81,9 @@ def tile_list_cheat_review_queue_kernel(
         wg = [wg_first[:]] + [wg_rest[:, j, :] for j in range(PACK - 1)]
 
         state_rows = state.rearrange("(p j) t -> p j t", j=PACK)
-        z = [[sb("z%d_%d" % (u, c), [P, 2, BANK], F32) for c in range(chunks)] for u in range(2)]
-
-        def load_state(u):
-            for c in range(chunks):
-                nc.sync.dma_start(z[u][c][:], state_rows[:, 2 * u : 2 * u + 2, c * BANK : (c + 1) * BANK])
+        z_lo = sb("z_lo", [P, 2, T2], F32)
+        z_hi = [sb("z_hi%d" % c, [P, 2, BANK], F32) for c in range(chunks)]
+        z = [[z_lo[:, :, c * BANK : (c + 1) * BANK] for c in range(chunks)], [tl[:] for tl in z_hi]]
 
         wb_raw = sb("wb_raw", [P, PACK, N], F32, tag="wb_raw")
         nc.sync.dma_start(wb_raw[:], wb.rearrange("(p j) n -> p j n", j=PACK))
@@ -94,8 +92,12 @@ def tile_list_cheat_review_queue_kernel(
             nc.sync.dma_start(rs_sb[:], rs.rearrange("(i p) -> p i", p=P))
         wgo_sb = sb("wgo_sb", [P, PICKS], F32)
         nc.sync.dma_start(wgo_sb[:], wgo)
-        load_state(0)
-        load_state(1)
+        for j in range(2):
+            nc.sync.dma_start(z_lo[:, j, :], state_rows[:, j, :])
+        for c in range(chunks):
+            nc.sync.dma_start(z_hi[c][:], state_rows[:, 2:4, c * BANK : (c + 1) * BANK])
+        nc.sync.dma_start(idx_pick[:], offs3)
+        nc.sync.dma_start(idx_out[:], offs4)
         wa_codes = sb("wa_codes", [P, 2 * N], U8)
         nc.sync.dma_start(wa_codes[:].bitcast(I32), wa_words[0].bitcast(I32))
         wa_sc = sb("wa_sc", [P, N], U8)
@@ -109,30 +111,25 @@ def tile_list_cheat_review_queue_kernel(
         nc.scalar.activation(zero[:], zero_in[:], ACT.Silu)
 
         pages = [sb("page%d" % b, [P, T2], F32) for b in range(2)]
-        outs = [sb("out%d" % b, [P, T2], F32) for b in range(2)]
-        for tl in pages + outs:
+        for tl in pages:
             nc.vector.memset(tl[:], 0.0)
 
         v_codes = [sb("v_codes0", [P, S], U32)]
         v_sc = sb("v_sc", [P, S], U8)
-        nc.vector.tensor_copy(v_codes[0][:], tab[0][:].indirect(idx_tab[:]))
         nc.vector.tensor_copy(v_sc[:], tab_sc[:].indirect(idx_tab[:]))
+        nc.vector.tensor_copy(v_codes[0][:], tab[0][:].indirect(idx_tab[:]))
 
         w1_codes = sb("w1_codes", [P, passes, H], U32)
         w1_sc = sb("w1_sc", [P, passes, H], U8)
         for a in range(passes):
-            w1_bf = sb("w1_bf%d" % a, [P, PACK * H], BF16, tag=("big2", "tab_sc")[a])
+            w1_bf = sb("w1_bf%d" % a, [P, PACK * H], BF16, tag=("big2", "zz_bf3")[a])
             dst = w1_bf[:].rearrange("p (t m j) -> p m j t", t=PACK, j=PACK)
             src = w1_raw[a][:].rearrange("p j (m t) -> p m j t", t=PACK)
-            if a == 0:
-                nc.scalar.copy(dst, src)
-            else:
-                nc.vector.tensor_copy(dst, src)
+            nc.scalar.copy(dst, src)
             nc.vector.quantize_mx(w1_codes[:, a, :].bitcast(FP8X4), w1_sc[:, a, :], w1_bf[:])
         v_codes.append(sb("v_codes1", [P, S], U32, tag="tab_sc"))
 
-        x_banks = [four_banks(u, "x%d" % u) for u in range(2)]
-        x = [[x_banks[j // 2][:, halves * (j % 2) + h, :] for h in range(halves)] for j in range(PACK)]
+        x = [[bank(halves * j + h, "x%d_%d" % (j, h))[:] for h in range(halves)] for j in range(PACK)]
 
         def stage1(a, j, h):
             cols = slice(h * BANK, (h + 1) * BANK)
@@ -155,54 +152,62 @@ def tile_list_cheat_review_queue_kernel(
                 for a in range(passes):
                     stage1(a, j, h)
 
+        outs = [sb("out%d" % b, [P, T2], F32, tag="tab%d" % b) for b in range(2)]
+        for tl in outs:
+            nc.gpsimd.memset(tl[:], 0.0)
+
         sines = [sb("sine%d" % j, [P, S], F32, tag="slot%d" % j) for j in range(PACK)]
 
-        def sine(j, h):
-            turns = ring.tile([P, BANK], F32, name="turns", tag="ring_a", align_bytes=64)
-            whole = ring.tile([P, BANK], U32, name="whole", tag="ring_b", align_bytes=64)
-            nc.scalar.activation(turns[:], x[j][h], ACT.Copy, scale=1.0 / TWO_PI)
-            nc.scalar.activation(whole[:], turns[:], ACT.Copy, bias=ROUNDER)
-            nc.vector.scalar_tensor_tensor(
-                turns[:], whole[:].bitcast(I32), ROUNDER, turns[:], ALU.subtract, ALU.subtract
-            )
-            nc.scalar.activation(sines[j][:, h * BANK : (h + 1) * BANK], turns[:], ACT.Sin, bias=zero[:], scale=-TWO_PI)
+        def fraction(j, h):
+            turns = sines[j][:, h * BANK : (h + 1) * BANK]
+            whole = ring.tile([P, BANK], U32, name="whole", align_bytes=64)
+            nc.scalar.activation(turns, x[j][h], ACT.Copy, scale=1.0 / TWO_PI)
+            nc.scalar.activation(whole[:], turns, ACT.Copy, bias=ROUNDER)
+            nc.vector.scalar_tensor_tensor(turns, whole[:].bitcast(I32), ROUNDER, turns, ALU.subtract, ALU.subtract)
+
+        def sine(j, lo, hi):
+            nc.scalar.activation(sines[j][:, lo:hi], sines[j][:, lo:hi], ACT.Sin, bias=zero[:], scale=-TWO_PI)
 
         def scatter(j, lo, hi):
             nc.vector.tensor_tensor(
-                pages[j % 2][:].indirect(idx_page[:, lo // 16 : hi // 16]), sines[j][:, lo:hi], wg[j][:, lo:hi], ALU.mult
+                pages[min(j, 1)][:].indirect(idx_page[:, lo // 16 : hi // 16]), sines[j][:, lo:hi], wg[j][:, lo:hi], ALU.mult
             )
 
-        def add_state(j, c):
-            zj = z[j // 2][c][:, j % 2, :]
-            nc.vector.scalar_tensor_tensor(
-                zj, pages[j % 2][:, c * BANK : (c + 1) * BANK], gain_sb[:, j : j + 1], zj, ALU.mult, ALU.add
-            )
+        def add_state(j, zj, cols):
+            nc.vector.scalar_tensor_tensor(zj, pages[min(j, 1)][:, cols], gain_sb[:, j : j + 1], zj, ALU.mult, ALU.add)
+
+        def add_chunk(j, c):
+            add_state(j, z_hi[c][:, j - 2, :], slice(c * BANK, (c + 1) * BANK))
 
         z_bf = [sb("z_bf%d" % c, [P, BANK, PACK], BF16) for c in range(chunks)]
         zz_bf = [sb("zz_bf%d" % c, [P, BANK, PACK], BF16) for c in range(chunks)]
 
         def round_pair(u, c):
-            src = z[u][c][:].rearrange("p j t -> p t j")
+            src = z[u][c].rearrange("p j t -> p t j")
             if u == 0:
                 nc.scalar.copy(z_bf[c][:, :, 0:2], src)
             else:
                 nc.vector.tensor_copy(z_bf[c][:, :, 2:4], src)
             nc.scalar.activation(zz_bf[c][:, :, 2 * u : 2 * u + 2], src, ACT.Square)
 
-        sine(0, 0)
-        sine(0, 1)
-        scatter(0, 0, BANK)
-        sine(1, 0)
-        sine(1, 1)
-        scatter(0, BANK, S)
+        for h in range(halves):
+            fraction(0, h)
+        for h in range(halves):
+            sine(0, h * BANK, (h + 1) * BANK)
+            scatter(0, h * BANK, (h + 1) * BANK)
+        for j in range(1, PACK):
+            for h in range(halves):
+                fraction(j, h)
+        for j in range(1, PACK):
+            sine(j, 0, S)
         for j in range(PACK - 1):
-            if j + 2 < PACK:
-                sine(j + 2, 0)
-                sine(j + 2, 1)
-            for c in range(chunks):
-                add_state(j, c)
+            if j < 2:
+                add_state(j, z_lo[:, j, :], slice(0, T2))
+            else:
+                for c in range(chunks):
+                    add_chunk(j, c)
             scatter(j + 1, 0, S)
-            if j == 0:
+            if j == 1:
                 wb_bf = sb("wb_bf", [P, N, PACK], BF16)
                 nc.scalar.copy(
                     wb_bf[:].rearrange("p (c i) j -> p c j i", i=4), wb_raw[:].rearrange("p j (c i) -> p c j i", i=4)
@@ -224,8 +229,8 @@ def tile_list_cheat_review_queue_kernel(
         scales = [sb("scales%d" % c, [P, 2, BANK], U8) for c in range(chunks)]
         scores = [sb("score%d" % i, [P, T2], F32, tag="big%d" % i) for i in range(n_tiles)]
 
-        def stage2(i, c, y_banks):
-            acc = y_banks[:, c, :]
+        def stage2(i, c):
+            acc = bank(c if i == 0 else chunks - 1 - c % 2, "y%d_%d" % (i, c))[:]
             rows = slice(i * P, (i + 1) * P)
             nc.tensor.matmul_mx(
                 acc,
@@ -247,23 +252,23 @@ def tile_list_cheat_review_queue_kernel(
             )
             nc.scalar.activation(scores[i][:, c * BANK : (c + 1) * BANK], acc, ACT.Tanh, bias=zero[:])
 
-        y_banks = four_banks(0, "y0")
         for c in range(chunks):
-            add_state(PACK - 1, c)
+            add_chunk(PACK - 1, c)
+        for c in range(chunks):
             round_pair(1, c)
+        for c in range(chunks):
             for u, src in enumerate((z_bf[c], zz_bf[c])):
                 nc.vector.quantize_mx(
                     codes[c][:, u, :].bitcast(FP8X4), scales[c][:, u, :], src[:].rearrange("p t j -> p (t j)")
                 )
-            stage2(0, c, y_banks)
+            stage2(0, c)
         for i in range(1, n_tiles):
-            y_banks = four_banks(0, "y%d" % i)
             for c in range(chunks):
-                stage2(i, c, y_banks)
+                stage2(i, c)
 
         factors = [factor0[:]]
         for i in range(n_tiles):
-            picked = sb("picked%d" % i, [P, PICKS], F32, tag="z0_%d" % i)
+            picked = sb("picked%d" % i, [P, PICKS], F32, tag="z_bf%d" % i)
             nc.vector.tensor_copy(picked[:], scores[i][:].indirect(idx_pick[:]))
             if i == 0:
                 factor_rest = sb("factor_rest", [P, n_tiles - 1, PICKS], F32, tag="big0")

@@ -36,7 +36,7 @@ def tile_list_cheat_review_queue_kernel(
     with ExitStack() as ctx:
         lists = ctx.enter_context(tc.tile_pool(name="lists", bufs=1))
         keep = ctx.enter_context(tc.tile_pool(name="keep", bufs=1))
-        ring = ctx.enter_context(tc.tile_pool(name="ring", bufs=6))
+        ring = ctx.enter_context(tc.tile_pool(name="ring", bufs=7))
         psum = ctx.enter_context(tc.psum_pool(name="psum", bufs=1))
 
         def sb(name, shape, dtype, tag=None):
@@ -69,22 +69,24 @@ def tile_list_cheat_review_queue_kernel(
             nc.vector.tensor_copy(tab_sc[rows, :].bitcast(I32), sc_rows[rows, :])
 
         wgs_rows = wgs.rearrange("(m j) s -> m j s", j=PACK)
-        wg_first = sb("wg_first", [P, S], F32)
-        wg_rest = sb("wg_rest", [P, PACK - 1, S], F32)
-        for q in range(4):
-            nc.sync.dma_start(wg_first[32 * q : 32 * q + 32, :], wgs_rows[:, 0, :])
+        wg = [sb("wg%d" % j, [P, S], F32) for j in range(PACK)]
+
+        def load_wg(j):
+            for q in (0, 2, 1, 3):
+                nc.sync.dma_start(wg[j][32 * q : 32 * q + 32, :], wgs_rows[:, j, :])
+
+        load_wg(0)
         nc.sync.dma_start(idx_page[:], offs2)
         gain_sb = sb("gain_sb", [P, PACK], F32)
         nc.sync.dma_start(gain_sb[:], gain.rearrange("(p j) -> p j", j=PACK))
-        for q in range(4):
-            nc.sync.dma_start(wg_rest[32 * q : 32 * q + 32, :, :], wgs_rows[:, 1:PACK, :])
-        wg = [wg_first[:]] + [wg_rest[:, j, :] for j in range(PACK - 1)]
+        load_wg(1)
 
         state_rows = state.rearrange("(p j) t -> p j t", j=PACK)
         z_lo = sb("z_lo", [P, 2, T2], F32)
         z_hi = [sb("z_hi%d" % c, [P, 2, BANK], F32) for c in range(chunks)]
         z = [[z_lo[:, :, c * BANK : (c + 1) * BANK] for c in range(chunks)], [tl[:] for tl in z_hi]]
 
+        nc.sync.dma_start(z_lo[:, 0, :], state_rows[:, 0, :])
         wb_raw = sb("wb_raw", [P, PACK, N], F32, tag="wb_raw")
         nc.sync.dma_start(wb_raw[:], wb.rearrange("(p j) n -> p j n", j=PACK))
         rs_sb = sb("rs_sb", [P, n_tiles], F32)
@@ -92,10 +94,11 @@ def tile_list_cheat_review_queue_kernel(
             nc.sync.dma_start(rs_sb[:], rs.rearrange("(i p) -> p i", p=P))
         wgo_sb = sb("wgo_sb", [P, PICKS], F32)
         nc.sync.dma_start(wgo_sb[:], wgo)
-        for j in range(2):
-            nc.sync.dma_start(z_lo[:, j, :], state_rows[:, j, :])
+        nc.sync.dma_start(z_lo[:, 1, :], state_rows[:, 1, :])
+        load_wg(2)
         for c in range(chunks):
             nc.sync.dma_start(z_hi[c][:], state_rows[:, 2:4, c * BANK : (c + 1) * BANK])
+        load_wg(3)
         nc.sync.dma_start(idx_pick[:], offs3)
         nc.sync.dma_start(idx_out[:], offs4)
         wa_codes = sb("wa_codes", [P, 2 * N], U8)
@@ -112,7 +115,7 @@ def tile_list_cheat_review_queue_kernel(
 
         pages = [sb("page%d" % b, [P, T2], F32) for b in range(2)]
         for tl in pages:
-            nc.vector.memset(tl[:], 0.0)
+            nc.vector.memset(tl[:].bitcast(I32), 0)
 
         v_codes = [sb("v_codes0", [P, S], U32)]
         v_sc = sb("v_sc", [P, S], U8)
@@ -152,16 +155,16 @@ def tile_list_cheat_review_queue_kernel(
                 for a in range(passes):
                     stage1(a, j, h)
 
-        outs = [sb("out%d" % b, [P, T2], F32, tag="tab%d" % b) for b in range(2)]
+        outs = [sb("out%d" % b, [P, T2], F32) for b in range(2)]
         for tl in outs:
-            nc.gpsimd.memset(tl[:], 0.0)
+            nc.vector.memset(tl[:].bitcast(I32), 0)
 
         sines = [sb("sine%d" % j, [P, S], F32, tag="slot%d" % j) for j in range(PACK)]
 
-        def fraction(j, h):
-            turns = sines[j][:, h * BANK : (h + 1) * BANK]
-            whole = ring.tile([P, BANK], U32, name="whole", align_bytes=64)
-            nc.scalar.activation(turns, x[j][h], ACT.Copy, scale=1.0 / TWO_PI)
+        def fraction(j, lo, hi):
+            turns = sines[j][:, lo:hi]
+            whole = ring.tile([P, hi - lo], U32, name="whole", align_bytes=64)
+            nc.scalar.activation(turns, x[j][lo // BANK][:, lo % BANK : lo % BANK + hi - lo], ACT.Copy, scale=1.0 / TWO_PI)
             nc.scalar.activation(whole[:], turns, ACT.Copy, bias=ROUNDER)
             nc.vector.scalar_tensor_tensor(turns, whole[:].bitcast(I32), ROUNDER, turns, ALU.subtract, ALU.subtract)
 
@@ -182,22 +185,19 @@ def tile_list_cheat_review_queue_kernel(
         z_bf = [sb("z_bf%d" % c, [P, BANK, PACK], BF16) for c in range(chunks)]
         zz_bf = [sb("zz_bf%d" % c, [P, BANK, PACK], BF16) for c in range(chunks)]
 
-        def round_pair(u, c):
-            src = z[u][c].rearrange("p j t -> p t j")
-            if u == 0:
-                nc.scalar.copy(z_bf[c][:, :, 0:2], src)
-            else:
-                nc.vector.tensor_copy(z_bf[c][:, :, 2:4], src)
-            nc.scalar.activation(zz_bf[c][:, :, 2 * u : 2 * u + 2], src, ACT.Square)
+        def round_z(u, c, copy):
+            copy(z_bf[c][:, :, 2 * u : 2 * u + 2], z[u][c].rearrange("p j t -> p t j"))
 
-        for h in range(halves):
-            fraction(0, h)
-        for h in range(halves):
-            sine(0, h * BANK, (h + 1) * BANK)
-            scatter(0, h * BANK, (h + 1) * BANK)
+        def round_square(u, c):
+            nc.scalar.activation(zz_bf[c][:, :, 2 * u : 2 * u + 2], z[u][c].rearrange("p j t -> p t j"), ACT.Square)
+
+        for lo, hi in ((0, BANK // 2), (BANK // 2, BANK), (BANK, S)):
+            fraction(0, lo, hi)
+            sine(0, lo, hi)
+            scatter(0, lo, hi)
         for j in range(1, PACK):
             for h in range(halves):
-                fraction(j, h)
+                fraction(j, h * BANK, (h + 1) * BANK)
         for j in range(1, PACK):
             sine(j, 0, S)
         for j in range(PACK - 1):
@@ -223,7 +223,8 @@ def tile_list_cheat_review_queue_kernel(
                 nc.scalar.activation(factor0[:], wgo_sb[:], ACT.Copy, scale=rs_sb[:, 0:1])
             if j == 1:
                 for c in range(chunks):
-                    round_pair(0, c)
+                    round_z(0, c, nc.scalar.copy)
+                    round_square(0, c)
 
         codes = [sb("codes%d" % c, [P, 2, BANK], U32, tag="slot%d" % c) for c in range(chunks)]
         scales = [sb("scales%d" % c, [P, 2, BANK], U8) for c in range(chunks)]
@@ -255,7 +256,9 @@ def tile_list_cheat_review_queue_kernel(
         for c in range(chunks):
             add_chunk(PACK - 1, c)
         for c in range(chunks):
-            round_pair(1, c)
+            round_square(1, c)
+        for c in range(chunks):
+            round_z(1, c, nc.vector.tensor_copy if c < chunks - 1 else nc.scalar.copy)
         for c in range(chunks):
             for u, src in enumerate((z_bf[c], zz_bf[c])):
                 nc.vector.quantize_mx(

@@ -2,6 +2,7 @@ import math
 from contextlib import ExitStack
 
 import concourse.mybir as mybir
+from concourse.masks import make_identity
 
 K, H, N, T, S, T2, PICKS = 1024, 512, 384, 4096, 1024, 2048, 1024
 FLOPS = 2 * K * H * S + 2 * 2 * H * N * T2
@@ -36,7 +37,7 @@ def tile_list_cheat_review_queue_kernel(
     with ExitStack() as ctx:
         lists = ctx.enter_context(tc.tile_pool(name="lists", bufs=1))
         keep = ctx.enter_context(tc.tile_pool(name="keep", bufs=1))
-        ring = ctx.enter_context(tc.tile_pool(name="ring", bufs=7))
+        ring = ctx.enter_context(tc.tile_pool(name="ring", bufs=2))
         psum = ctx.enter_context(tc.psum_pool(name="psum", bufs=1))
 
         def sb(name, shape, dtype, tag=None):
@@ -134,42 +135,62 @@ def tile_list_cheat_review_queue_kernel(
 
         x = [[bank(halves * j + h, "x%d_%d" % (j, h))[:] for h in range(halves)] for j in range(PACK)]
 
+        blocks = BANK // P
+
         def stage1(a, j, h):
-            cols = slice(h * BANK, (h + 1) * BANK)
             rows = slice(j * P, (j + 1) * P)
-            nc.tensor.matmul_mx(
-                x[j][h],
-                lhsT=w1_codes[:, a, rows].bitcast(FP8X4),
-                lhsT_scale=w1_sc[:, a, rows],
-                rhs=v_codes[a][:, cols].bitcast(FP8X4),
-                rhs_scale=v_sc[4 * a : P, cols],
-                start=(a == 0),
-                stop=(a == passes - 1),
-            )
+            for b in range(blocks):
+                cols = slice(h * BANK + b * P, h * BANK + (b + 1) * P)
+                nc.tensor.matmul_mx(
+                    x[j][h][:, b * P : (b + 1) * P],
+                    lhsT=v_codes[a][:, cols].bitcast(FP8X4),
+                    lhsT_scale=v_sc[4 * a : P, cols],
+                    rhs=w1_codes[:, a, rows].bitcast(FP8X4),
+                    rhs_scale=w1_sc[:, a, rows],
+                    start=(a == 0 and b == 0),
+                    stop=(a == passes - 1 and b == blocks - 1),
+                )
 
         for h in range(halves):
             nc.vector.tensor_copy(
                 v_codes[1][:, h * BANK : (h + 1) * BANK], tab[1][:].indirect(idx_tab[:, h * 32 : (h + 1) * 32])
             )
-            for j in range(PACK):
-                for a in range(passes):
-                    stage1(a, j, h)
 
-        outs = [sb("out%d" % b, [P, T2], F32) for b in range(2)]
+        ident = sb("ident", [P, P], F32)
+        make_identity(nc, ident[:])
+
+        outs = [sb("out%d" % b, [P, T2], F32, tag=("tab0", "big2")[b]) for b in range(2)]
         for tl in outs:
             nc.vector.memset(tl[:].bitcast(I32), 0)
 
         sines = [sb("sine%d" % j, [P, S], F32, tag="slot%d" % j) for j in range(PACK)]
 
-        def fraction(j, lo, hi):
-            turns = sines[j][:, lo:hi]
-            whole = ring.tile([P, hi - lo], U32, name="whole", align_bytes=64)
-            nc.scalar.activation(turns, x[j][lo // BANK][:, lo % BANK : lo % BANK + hi - lo], ACT.Copy, scale=1.0 / TWO_PI)
-            nc.scalar.activation(whole[:], turns, ACT.Copy, bias=ROUNDER)
-            nc.vector.scalar_tensor_tensor(turns, whole[:].bitcast(I32), ROUNDER, turns, ALU.subtract, ALU.subtract)
-
-        def sine(j, lo, hi):
-            nc.scalar.activation(sines[j][:, lo:hi], sines[j][:, lo:hi], ACT.Sin, bias=zero[:], scale=-TWO_PI)
+        def sine(j, h, pieces, after_piece):
+            turns = ring.tile([P, BANK], F32, name="turns", bufs=3, align_bytes=64)
+            shifted = ring.tile([P, BANK], U32, name="shifted", tag="shifted", align_bytes=64)
+            whole = ring.tile([P, BANK], F32, name="whole", align_bytes=64)
+            for a in range(passes):
+                stage1(a, j, h)
+            nc.scalar.activation(turns[:], x[j][h], ACT.Copy, scale=-1.0 / TWO_PI)
+            rest = bank(halves * j + h, "rest%d_%d" % (j, h))
+            width = BANK // pieces
+            for lo in range(0, BANK, width):
+                cols = slice(lo, lo + width)
+                nc.scalar.activation(shifted[:, cols], turns[:, cols], ACT.Copy, bias=ROUNDER, scale=-1.0)
+                nc.scalar.activation(whole[:, cols], shifted[:, cols], ACT.Copy, bias=-ROUNDER)
+                for term in (turns, whole):
+                    for b in range(lo, lo + width, P):
+                        nc.tensor.matmul(
+                            rest[:, b : b + P],
+                            lhsT=term[:, b : b + P],
+                            rhs=ident[:],
+                            is_transpose=True,
+                            start=(term is turns and b == lo),
+                            stop=(term is whole and b + P == lo + width),
+                        )
+                done = slice(h * BANK + lo, h * BANK + lo + width)
+                nc.scalar.activation(sines[j][:, done], rest[:, cols], ACT.Sin, bias=zero[:], scale=-TWO_PI)
+                after_piece(j, done.start, done.stop)
 
         def scatter(j, lo, hi):
             nc.vector.tensor_tensor(
@@ -191,15 +212,11 @@ def tile_list_cheat_review_queue_kernel(
         def round_square(u, c):
             nc.scalar.activation(zz_bf[c][:, :, 2 * u : 2 * u + 2], z[u][c].rearrange("p j t -> p t j"), ACT.Square)
 
-        for lo, hi in ((0, BANK // 2), (BANK // 2, BANK), (BANK, S)):
-            fraction(0, lo, hi)
-            sine(0, lo, hi)
-            scatter(0, lo, hi)
+        sine(0, 0, 2, scatter)
+        sine(0, 1, 1, scatter)
         for j in range(1, PACK):
             for h in range(halves):
-                fraction(j, h * BANK, (h + 1) * BANK)
-        for j in range(1, PACK):
-            sine(j, 0, S)
+                sine(j, h, 1, lambda *unused: None)
         for j in range(PACK - 1):
             if j < 2:
                 add_state(j, z_lo[:, j, :], slice(0, T2))
@@ -208,7 +225,7 @@ def tile_list_cheat_review_queue_kernel(
                     add_chunk(j, c)
             scatter(j + 1, 0, S)
             if j == 1:
-                wb_bf = sb("wb_bf", [P, N, PACK], BF16)
+                wb_bf = ring.tile([P, N, PACK], BF16, name="wb_bf", tag="shifted", align_bytes=64)
                 nc.scalar.copy(
                     wb_bf[:].rearrange("p (c i) j -> p c j i", i=4), wb_raw[:].rearrange("p j (c i) -> p c j i", i=4)
                 )
@@ -219,8 +236,6 @@ def tile_list_cheat_review_queue_kernel(
                     nc.vector.quantize_mx(
                         wb_codes[:, lo:hi].bitcast(FP8X4), wb_sc[:, lo:hi], wb_flat[:, PACK * lo : PACK * hi]
                     )
-                factor0 = sb("factor0", [P, PICKS], F32, tag="wb_raw")
-                nc.scalar.activation(factor0[:], wgo_sb[:], ACT.Copy, scale=rs_sb[:, 0:1])
             if j == 1:
                 for c in range(chunks):
                     round_z(0, c, nc.scalar.copy)
@@ -228,7 +243,7 @@ def tile_list_cheat_review_queue_kernel(
 
         codes = [sb("codes%d" % c, [P, 2, BANK], U32, tag="slot%d" % c) for c in range(chunks)]
         scales = [sb("scales%d" % c, [P, 2, BANK], U8) for c in range(chunks)]
-        scores = [sb("score%d" % i, [P, T2], F32, tag="big%d" % i) for i in range(n_tiles)]
+        scores = [sb("score%d" % i, [P, T2], F32, tag=("big0", "big1", "score2")[i]) for i in range(n_tiles)]
 
         def stage2(i, c):
             acc = bank(c if i == 0 else chunks - 1 - c % 2, "y%d_%d" % (i, c))[:]
@@ -265,6 +280,8 @@ def tile_list_cheat_review_queue_kernel(
                     codes[c][:, u, :].bitcast(FP8X4), scales[c][:, u, :], src[:].rearrange("p t j -> p (t j)")
                 )
             stage2(0, c)
+        factor0 = sb("factor0", [P, PICKS], F32, tag="wb_raw")
+        nc.scalar.activation(factor0[:], wgo_sb[:], ACT.Copy, scale=rs_sb[:, 0:1])
         for i in range(1, n_tiles):
             for c in range(chunks):
                 stage2(i, c)

@@ -48,11 +48,11 @@ def tile_list_cheat_review_queue_kernel(
 
         idx_tab, idx_page, idx_pick, idx_out = [lists.tile([P, S // 16], U16, name="list%d" % n) for n in range(4)]
         sc_rows = sb("sc_rows", [P, T // 4], I32, tag="slot3")
-        for q in range(4):
-            nc.sync.dma_start(
-                sc_rows[32 * q : 32 * q + 4 * passes, :], tab_scales[:, 4 * q : 4 * q + 4, :].bitcast(I32)
-            )
-        nc.sync.dma_start(idx_tab[:], offs)
+
+        def load_scale_rows(rows):
+            for r in rows:
+                for a in range(passes):
+                    nc.sync.dma_start(sc_rows[4 * a + r : P : 32, :], tab_scales[a, r:16:4, :].bitcast(I32))
 
         tab = [sb("tab%d" % a, [P, T], U32) for a in range(passes)]
 
@@ -61,7 +61,12 @@ def tile_list_cheat_review_queue_kernel(
 
         w1_raw = [sb("w1_raw%d" % a, [P, PACK, H], F32, tag="big%d" % a) for a in range(passes)]
         for a in range(passes):
+            if a == 0:
+                load_scale_rows((0, 1))
             nc.sync.dma_start(w1_raw[a][:], w1[a * 512 : (a + 1) * 512, :].rearrange("(p j) c -> p j c", j=PACK))
+            if a == 0:
+                load_scale_rows((2, 3))
+                nc.sync.dma_start(idx_tab[:], offs)
             load_tab(a)
         tab_sc = sb("tab_sc", [P, T], U8)
         nc.vector.memset(tab_sc[:].bitcast(I32), 0)
@@ -194,11 +199,11 @@ def tile_list_cheat_review_queue_kernel(
 
         def scatter(j, lo, hi):
             nc.vector.tensor_tensor(
-                pages[min(j, 1)][:].indirect(idx_page[:, lo // 16 : hi // 16]), sines[j][:, lo:hi], wg[j][:, lo:hi], ALU.mult
+                pages[j % 2][:].indirect(idx_page[:, lo // 16 : hi // 16]), sines[j][:, lo:hi], wg[j][:, lo:hi], ALU.mult
             )
 
         def add_state(j, zj, cols):
-            nc.vector.scalar_tensor_tensor(zj, pages[min(j, 1)][:, cols], gain_sb[:, j : j + 1], zj, ALU.mult, ALU.add)
+            nc.vector.scalar_tensor_tensor(zj, pages[j % 2][:, cols], gain_sb[:, j : j + 1], zj, ALU.mult, ALU.add)
 
         def add_chunk(j, c):
             add_state(j, z_hi[c][:, j - 2, :], slice(c * BANK, (c + 1) * BANK))

import math
from contextlib import ExitStack

import concourse.mybir as mybir
from concourse.masks import make_identity

K, H, N, T, S, T2, PICKS = 1024, 512, 384, 4096, 1024, 2048, 1024
FLOPS = 2 * K * H * S + 2 * 2 * H * N * T2

F32 = mybir.dt.float32
BF16 = mybir.dt.bfloat16
I32 = mybir.dt.int32
U32 = mybir.dt.uint32
U16 = mybir.dt.uint16
U8 = mybir.dt.uint8
FP8X4 = mybir.dt.float8_e4m3fn_x4
FP4X4 = mybir.dt.float4_e2m1fn_x4
ACT = mybir.ActivationFunctionType
ALU = mybir.AluOpType

P = 128
PACK = 4
BANK = 512
ROUNDER = 1.5 * 2.0**23
TWO_PI = 2.0 * math.pi


def tile_list_cheat_review_queue_kernel(
    tc, tab_words, tab_scales, w1, gain, state, wa_words, wa_scales, wb, rs, wgs, wgo, offs, offs2, offs3, offs4, out
):
    nc = tc.nc
    passes = K // (P * PACK)
    halves = S // BANK
    chunks = T2 // BANK
    n_tiles = N // P

    with ExitStack() as ctx:
        lists = ctx.enter_context(tc.tile_pool(name="lists", bufs=1))
        keep = ctx.enter_context(tc.tile_pool(name="keep", bufs=1))
        ring = ctx.enter_context(tc.tile_pool(name="ring", bufs=2))
        psum = ctx.enter_context(tc.psum_pool(name="psum", bufs=1))

        def sb(name, shape, dtype, tag=None):
            return keep.tile(shape, dtype, name=name, tag=tag or name, align_bytes=64)

        def bank(b, name):
            return psum.tile([P, BANK], F32, name=name, tag="bank%d" % b)

        idx_tab, idx_page, idx_pick, idx_out = [lists.tile([P, S // 16], U16, name="list%d" % n) for n in range(4)]
        sc_rows = sb("sc_rows", [P, T // 4], I32, tag="slot3")

        def load_scale_rows(rows):
            for r in rows:
                for a in range(passes):
                    nc.sync.dma_start(sc_rows[4 * a + r : P : 32, :], tab_scales[a, r:16:4, :].bitcast(I32))

        tab = [sb("tab%d" % a, [P, T], U32) for a in range(passes)]

        def load_tab(a):
            nc.sync.dma_start(tab[a][:].bitcast(I32), tab_words[a].rearrange("p t i -> p (t i)").bitcast(I32))

        w1_raw = [sb("w1_raw%d" % a, [P, PACK, H], F32, tag="big%d" % a) for a in range(passes)]
        for a in range(passes):
            if a == 0:
                load_scale_rows((0, 1))
            nc.sync.dma_start(w1_raw[a][:], w1[a * 512 : (a + 1) * 512, :].rearrange("(p j) c -> p j c", j=PACK))
            if a == 0:
                load_scale_rows((2, 3))
                nc.sync.dma_start(idx_tab[:], offs)
            load_tab(a)
        tab_sc = sb("tab_sc", [P, T], U8)
        nc.vector.memset(tab_sc[:].bitcast(I32), 0)
        for q in range(4):
            rows = slice(32 * q, 32 * q + 4 * passes)
            nc.vector.tensor_copy(tab_sc[rows, :].bitcast(I32), sc_rows[rows, :])

        wgs_rows = wgs.rearrange("(m j) s -> m j s", j=PACK)
        wg = [sb("wg%d" % j, [P, S], F32) for j in range(PACK)]

        def load_wg(j):
            for q in (0, 2, 1, 3):
                nc.sync.dma_start(wg[j][32 * q : 32 * q + 32, :], wgs_rows[:, j, :])

        load_wg(0)
        nc.sync.dma_start(idx_page[:], offs2)
        gain_sb = sb("gain_sb", [P, PACK], F32)
        nc.sync.dma_start(gain_sb[:], gain.rearrange("(p j) -> p j", j=PACK))
        load_wg(1)

        state_rows = state.rearrange("(p j) t -> p j t", j=PACK)
        z_lo = sb("z_lo", [P, 2, T2], F32)
        z_hi = [sb("z_hi%d" % c, [P, 2, BANK], F32) for c in range(chunks)]
        z = [[z_lo[:, :, c * BANK : (c + 1) * BANK] for c in range(chunks)], [tl[:] for tl in z_hi]]

        nc.sync.dma_start(z_lo[:, 0, :], state_rows[:, 0, :])
        wb_raw = sb("wb_raw", [P, PACK, N], F32, tag="wb_raw")
        nc.sync.dma_start(wb_raw[:], wb.rearrange("(p j) n -> p j n", j=PACK))
        rs_sb = sb("rs_sb", [P, n_tiles], F32)
        with nc.allow_non_contiguous_dma(reason="one value of rs to a partition"):
            nc.sync.dma_start(rs_sb[:], rs.rearrange("(i p) -> p i", p=P))
        wgo_sb = sb("wgo_sb", [P, PICKS], F32)
        nc.sync.dma_start(wgo_sb[:], wgo)
        nc.sync.dma_start(z_lo[:, 1, :], state_rows[:, 1, :])
        load_wg(2)
        for c in range(chunks):
            nc.sync.dma_start(z_hi[c][:], state_rows[:, 2:4, c * BANK : (c + 1) * BANK])
        load_wg(3)
        nc.sync.dma_start(idx_pick[:], offs3)
        nc.sync.dma_start(idx_out[:], offs4)
        wa_codes = sb("wa_codes", [P, 2 * N], U8)
        nc.sync.dma_start(wa_codes[:].bitcast(I32), wa_words[0].bitcast(I32))
        wa_sc = sb("wa_sc", [P, N], U8)
        nc.vector.memset(wa_sc[:].bitcast(I32), 0)
        for q in range(4):
            nc.sync.dma_start(wa_sc[32 * q : 32 * q + 4, :].bitcast(I32), wa_scales[0, 4 * q : 4 * q + 4, :].bitcast(I32))

        zero_in = sb("zero_in", [P, 1], F32)
        zero = sb("zero", [P, 1], F32)
        nc.vector.memset(zero_in[:], 0.0)
        nc.scalar.activation(zero[:], zero_in[:], ACT.Silu)

        pages = [sb("page%d" % b, [P, T2], F32) for b in range(2)]
        for tl in pages:
            nc.vector.memset(tl[:].bitcast(I32), 0)

        v_codes = [sb("v_codes0", [P, S], U32)]
        v_sc = sb("v_sc", [P, S], U8)
        nc.vector.tensor_copy(v_sc[:], tab_sc[:].indirect(idx_tab[:]))
        nc.vector.tensor_copy(v_codes[0][:], tab[0][:].indirect(idx_tab[:]))

        w1_codes = sb("w1_codes", [P, passes, H], U32)
        w1_sc = sb("w1_sc", [P, passes, H], U8)
        for a in range(passes):
            w1_bf = sb("w1_bf%d" % a, [P, PACK * H], BF16, tag=("big2", "zz_bf3")[a])
            dst = w1_bf[:].rearrange("p (t m j) -> p m j t", t=PACK, j=PACK)
            src = w1_raw[a][:].rearrange("p j (m t) -> p m j t", t=PACK)
            nc.scalar.copy(dst, src)
            nc.vector.quantize_mx(w1_codes[:, a, :].bitcast(FP8X4), w1_sc[:, a, :], w1_bf[:])
        v_codes.append(sb("v_codes1", [P, S], U32, tag="tab_sc"))

        x = [[bank(halves * j + h, "x%d_%d" % (j, h))[:] for h in range(halves)] for j in range(PACK)]

        blocks = BANK // P

        def stage1(a, j, h):
            rows = slice(j * P, (j + 1) * P)
            for b in range(blocks):
                cols = slice(h * BANK + b * P, h * BANK + (b + 1) * P)
                nc.tensor.matmul_mx(
                    x[j][h][:, b * P : (b + 1) * P],
                    lhsT=v_codes[a][:, cols].bitcast(FP8X4),
                    lhsT_scale=v_sc[4 * a : P, cols],
                    rhs=w1_codes[:, a, rows].bitcast(FP8X4),
                    rhs_scale=w1_sc[:, a, rows],
                    start=(a == 0 and b == 0),
                    stop=(a == passes - 1 and b == blocks - 1),
                )

        for h in range(halves):
            nc.vector.tensor_copy(
                v_codes[1][:, h * BANK : (h + 1) * BANK], tab[1][:].indirect(idx_tab[:, h * 32 : (h + 1) * 32])
            )

        ident = sb("ident", [P, P], F32)
        make_identity(nc, ident[:])

        outs = [sb("out%d" % b, [P, T2], F32, tag=("tab0", "big2")[b]) for b in range(2)]
        for tl in outs:
            nc.vector.memset(tl[:].bitcast(I32), 0)

        sines = [sb("sine%d" % j, [P, S], F32, tag="slot%d" % j) for j in range(PACK)]

        def sine(j, h, pieces, after_piece):
            turns = ring.tile([P, BANK], F32, name="turns", bufs=3, align_bytes=64)
            shifted = ring.tile([P, BANK], U32, name="shifted", tag="shifted", align_bytes=64)
            whole = ring.tile([P, BANK], F32, name="whole", align_bytes=64)
            for a in range(passes):
                stage1(a, j, h)
            nc.scalar.activation(turns[:], x[j][h], ACT.Copy, scale=-1.0 / TWO_PI)
            rest = bank(halves * j + h, "rest%d_%d" % (j, h))
            width = BANK // pieces
            for lo in range(0, BANK, width):
                cols = slice(lo, lo + width)
                nc.scalar.activation(shifted[:, cols], turns[:, cols], ACT.Copy, bias=ROUNDER, scale=-1.0)
                nc.scalar.activation(whole[:, cols], shifted[:, cols], ACT.Copy, bias=-ROUNDER)
                for term in (turns, whole):
                    for b in range(lo, lo + width, P):
                        nc.tensor.matmul(
                            rest[:, b : b + P],
                            lhsT=term[:, b : b + P],
                            rhs=ident[:],
                            is_transpose=True,
                            start=(term is turns and b == lo),
                            stop=(term is whole and b + P == lo + width),
                        )
                done = slice(h * BANK + lo, h * BANK + lo + width)
                nc.scalar.activation(sines[j][:, done], rest[:, cols], ACT.Sin, bias=zero[:], scale=-TWO_PI)
                after_piece(j, done.start, done.stop)

        def scatter(j, lo, hi):
            nc.vector.tensor_tensor(
                pages[j % 2][:].indirect(idx_page[:, lo // 16 : hi // 16]), sines[j][:, lo:hi], wg[j][:, lo:hi], ALU.mult
            )

        def add_state(j, zj, cols):
            nc.vector.scalar_tensor_tensor(zj, pages[j % 2][:, cols], gain_sb[:, j : j + 1], zj, ALU.mult, ALU.add)

        def add_chunk(j, c):
            add_state(j, z_hi[c][:, j - 2, :], slice(c * BANK, (c + 1) * BANK))

        z_bf = [sb("z_bf%d" % c, [P, BANK, PACK], BF16) for c in range(chunks)]
        zz_bf = [sb("zz_bf%d" % c, [P, BANK, PACK], BF16) for c in range(chunks)]

        def round_z(u, c, copy):
            copy(z_bf[c][:, :, 2 * u : 2 * u + 2], z[u][c].rearrange("p j t -> p t j"))

        def round_square(u, c):
            nc.scalar.activation(zz_bf[c][:, :, 2 * u : 2 * u + 2], z[u][c].rearrange("p j t -> p t j"), ACT.Square)

        sine(0, 0, 2, scatter)
        sine(0, 1, 1, scatter)
        for j in range(1, PACK):
            for h in range(halves):
                sine(j, h, 1, lambda *unused: None)
        for j in range(PACK - 1):
            if j < 2:
                add_state(j, z_lo[:, j, :], slice(0, T2))
            else:
                for c in range(chunks):
                    add_chunk(j, c)
            scatter(j + 1, 0, S)
            if j == 1:
                wb_bf = ring.tile([P, N, PACK], BF16, name="wb_bf", tag="shifted", align_bytes=64)
                nc.scalar.copy(
                    wb_bf[:].rearrange("p (c i) j -> p c j i", i=4), wb_raw[:].rearrange("p j (c i) -> p c j i", i=4)
                )
                wb_codes = sb("wb_codes", [P, N], U32)
                wb_sc = sb("wb_sc", [P, N], U8)
                wb_flat = wb_bf[:].rearrange("p n j -> p (n j)")
                for lo, hi in ((0, 256), (256, N)):
                    nc.vector.quantize_mx(
                        wb_codes[:, lo:hi].bitcast(FP8X4), wb_sc[:, lo:hi], wb_flat[:, PACK * lo : PACK * hi]
                    )
            if j == 1:
                for c in range(chunks):
                    round_z(0, c, nc.scalar.copy)
                    round_square(0, c)

        codes = [sb("codes%d" % c, [P, 2, BANK], U32, tag="slot%d" % c) for c in range(chunks)]
        scales = [sb("scales%d" % c, [P, 2, BANK], U8) for c in range(chunks)]
        scores = [sb("score%d" % i, [P, T2], F32, tag=("big0", "big1", "score2")[i]) for i in range(n_tiles)]

        def stage2(i, c):
            acc = bank(c if i == 0 else chunks - 1 - c % 2, "y%d_%d" % (i, c))[:]
            rows = slice(i * P, (i + 1) * P)
            nc.tensor.matmul_mx(
                acc,
                lhsT=wa_codes[:, 2 * i * P : 2 * (i + 1) * P].bitcast(FP4X4),
                lhsT_scale=wa_sc[:, rows],
                rhs=codes[c][:, 0, :].bitcast(FP8X4),
                rhs_scale=scales[c][:, 0, :],
                start=True,
                stop=False,
            )
            nc.tensor.matmul_mx(
                acc,
                lhsT=wb_codes[:, rows].bitcast(FP8X4),
                lhsT_scale=wb_sc[:, rows],
                rhs=codes[c][:, 1, :].bitcast(FP8X4),
                rhs_scale=scales[c][:, 1, :],
                start=False,
                stop=True,
            )
            nc.scalar.activation(scores[i][:, c * BANK : (c + 1) * BANK], acc, ACT.Tanh, bias=zero[:])

        for c in range(chunks):
            add_chunk(PACK - 1, c)
        for c in range(chunks):
            round_square(1, c)
        for c in range(chunks):
            round_z(1, c, nc.vector.tensor_copy if c < chunks - 1 else nc.scalar.copy)
        for c in range(chunks):
            for u, src in enumerate((z_bf[c], zz_bf[c])):
                nc.vector.quantize_mx(
                    codes[c][:, u, :].bitcast(FP8X4), scales[c][:, u, :], src[:].rearrange("p t j -> p (t j)")
                )
            stage2(0, c)
        factor0 = sb("factor0", [P, PICKS], F32, tag="wb_raw")
        nc.scalar.activation(factor0[:], wgo_sb[:], ACT.Copy, scale=rs_sb[:, 0:1])
        for i in range(1, n_tiles):
            for c in range(chunks):
                stage2(i, c)

        factors = [factor0[:]]
        for i in range(n_tiles):
            picked = sb("picked%d" % i, [P, PICKS], F32, tag="z_bf%d" % i)
            nc.vector.tensor_copy(picked[:], scores[i][:].indirect(idx_pick[:]))
            if i == 0:
                factor_rest = sb("factor_rest", [P, n_tiles - 1, PICKS], F32, tag="big0")
                for m in range(1, n_tiles):
                    nc.scalar.activation(factor_rest[:, m - 1, :], wgo_sb[:], ACT.Copy, scale=rs_sb[:, m : m + 1])
                    factors.append(factor_rest[:, m - 1, :])
            nc.vector.tensor_tensor(outs[i % 2][:].indirect(idx_out[:]), picked[:], factors[i], ALU.mult)
            nc.sync.dma_start(out[i * P : (i + 1) * P, :], outs[i % 2][:])
